import numpy as np
import ml_dtypes


def mxq(x, axis, fmt="e4m3"):
    dtype, down = {"e4m3": (ml_dtypes.float8_e4m3fn, 7), "e5m2": (ml_dtypes.float8_e5m2, 14)}[fmt]
    v = np.moveaxis(np.asarray(x, np.float32).astype(ml_dtypes.bfloat16).astype(np.float64), axis, -1)
    blocks = v.reshape(v.shape[:-1] + (-1, 32))
    amax = np.abs(blocks).max(-1, keepdims=True)
    byte = np.maximum(np.where(amax > 0, np.frexp(amax)[1] - 1 + 127, 0) - down, 1)
    scale = np.exp2(byte - 127.0)
    codes = (blocks / scale).astype(np.float32).astype(dtype).astype(np.float64)
    return np.moveaxis((codes * scale).reshape(v.shape), -1, axis)


WIDE = False


def mx_kscale(k):
    if not WIDE:
        return np.ones(k)
    levels = np.array([10, -10, 5, -5, 0])
    if k % 512:
        return np.exp2(np.random.permutation(np.resize(levels, k // 32))).repeat(32)
    a = np.empty((k // 512, 16))
    for p in range(k // 512):
        a[p, :8] = np.random.permutation(np.resize(levels, 8))
        for g in range(8):
            far = levels[np.abs(levels - a[p, g]) >= 10]
            a[p, g + 8] = far[np.random.randint(len(far))]
    return np.exp2(a.ravel()).repeat(32)


def f64(x):
    return np.asarray(x).astype(np.float64)


def striped(idx):
    return np.tile(idx.reshape(-1, 16).T, (8, 1)).astype(np.uint16)


def unstriped(offs):
    return offs[:16].T.reshape(-1).astype(np.int64)


E2M1 = np.array([0.0, 0.5, 1.0, 1.5, 2.0, 3.0, 4.0, 6.0, -0.0, -0.5, -1.0, -1.5, -2.0, -3.0, -4.0, -6.0])


def pack_weight(w, fmt):
    k, n = w.shape
    w = f64(np.asarray(w, np.float32).astype(ml_dtypes.bfloat16)).reshape(k // 32, 32, n)
    amax = np.abs(w).max(1)
    if fmt == "e4m3":
        byte = np.frexp(amax)[1] - 1 + 127 - 7
    else:
        mant, ex = np.frexp(amax / 6.0)
        byte = np.where(mant > 0.5, ex, ex - 1) + 127
    byte = np.clip(np.where(amax > 0, byte, 1), 1, 254)
    scaled = (w * np.exp2(127.0 - byte)[:, None, :]).reshape(k, n).astype(np.float32)
    by_word = np.ascontiguousarray(scaled.reshape(k // 512, 128, 4, n).transpose(0, 1, 3, 2))
    if fmt == "e4m3":
        words = by_word.astype(ml_dtypes.float8_e4m3fn).view(np.uint8)
    else:
        c = by_word.astype(ml_dtypes.float4_e2m1fn).view(np.uint8) & 0xF
        words = (c[..., 0::2] | (c[..., 1::2] << 4)).reshape(k // 512, 128, 2 * n)
    return np.ascontiguousarray(words), np.ascontiguousarray(byte.astype(np.uint8).reshape(k // 512, 16, n))


def unpack_weight(words, scales, fmt):
    g, _, n = scales.shape
    words = np.ascontiguousarray(words).reshape(g, 128, n, -1)
    if fmt == "e4m3":
        vals = words.view(ml_dtypes.float8_e4m3fn).astype(np.float64)
    else:
        nib = np.empty((g, 128, n, 4), np.uint8)
        nib[..., 0::2] = words & 0xF
        nib[..., 1::2] = words >> 4
        vals = E2M1[nib]
    vals = vals * np.repeat(np.exp2(scales.astype(np.float64) - 127.0), 8, axis=1)[..., None]
    return vals.transpose(0, 1, 3, 2).reshape(g * 512, n)


def gelu(v):
    return 0.5 * v * (1.0 + np.tanh(np.sqrt(2.0 / np.pi) * (v + 0.044715 * v**3)))


def bf(x):
    return np.asarray(x, np.float32).astype(ml_dtypes.bfloat16)

def planes(Y):
    n, m = Y.shape
    b = f64(bf(Y)).reshape(n // 32, 32, m)
    amax = np.abs(b).max(1)
    byte = np.clip(np.where(amax > 0, np.frexp(amax)[1] - 1 + 127 - 7, 1), 1, 254)
    codes = (b * np.exp2(127.0 - byte)[:, None, :]).reshape(n, m).astype(np.float32).astype(ml_dtypes.float8_e4m3fn).view(np.uint8)
    words = codes.reshape(n // 512, 128, 4, m).transpose(0, 1, 3, 2)
    return np.ascontiguousarray(words), np.ascontiguousarray(byte.astype(np.uint8).reshape(n // 512, 16, m))


K, H, N, T, S = 1024, 512, 1024, 4096, 1024

def setup_inputs():
    n = np.random.standard_normal
    s = mx_kscale(K)[:, None]
    u = mx_kscale(H)[:, None]
    gain = np.exp(0.8 * n((1, N)))
    tab_words, tab_scales = pack_weight(n((K, T)) * s, "e4m3")
    w1 = (n((K, H)) / np.sqrt(K) / s * u.T).astype(np.float32)
    w2_words, w2_scales = pack_weight(n((K, H)) / np.sqrt(K) / s * u.T, "e2m1")
    w3_words, w3_scales = pack_weight(n((K, H)) / np.sqrt(K) / s * u.T, "e4m3")
    w4_words, w4_scales = pack_weight(n((H, N)) / np.sqrt(H) / u * gain, "e2m1")
    b4 = (0.5 * n(N) * gain[0]).astype(np.float32)
    return {"tab_words": tab_words, "tab_scales": tab_scales,
            "offs": striped(np.random.permutation(T)[:S]),
            "offs2": striped(np.random.permutation(T)[:S]),
            "offs3": striped(np.random.permutation(T)[:S]),
            "w1": w1, "w2_words": w2_words, "w2_scales": w2_scales,
            "w3_words": w3_words, "w3_scales": w3_scales,
            "w4_words": w4_words, "w4_scales": w4_scales, "b4": b4}

def reference(tab_words, tab_scales, offs, offs2, offs3, w1, w2_words, w2_scales,
              w3_words, w3_scales, w4_words, w4_scales, b4):
    va = unpack_weight(tab_words, tab_scales, "e4m3")[:, unstriped(offs)]
    vb = unpack_weight(tab_words, tab_scales, "e4m3")[:, unstriped(offs2)]
    vc = unpack_weight(tab_words, tab_scales, "e4m3")[:, unstriped(offs3)]
    a = mxq(f64(w1), 0, "e4m3").T @ va
    b = unpack_weight(w2_words, w2_scales, "e2m1").T @ vb
    c = unpack_weight(w3_words, w3_scales, "e4m3").T @ vc
    h = np.sqrt(np.abs(a * b)) - c
    y = (unpack_weight(w4_words, w4_scales, "e2m1").T @ mxq(h, 0, "e4m3")) + f64(b4)[:, None]
    words, scales = planes(y)
    return y, words, scales

@@ -1,0 +1,323 @@
+from contextlib import ExitStack
+
+import concourse.mybir as mybir
+
+K, H, N, T, S = 1024, 512, 1024, 4096, 1024
+FLOPS = 2 * (3 * K * H * S + H * N * S)
+
+F32 = mybir.dt.float32
+BF16 = mybir.dt.bfloat16
+I32 = mybir.dt.int32
+U32 = mybir.dt.uint32
+U16 = mybir.dt.uint16
+U8 = mybir.dt.uint8
+FP8X4 = mybir.dt.float8_e4m3fn_x4
+FP4X4 = mybir.dt.float4_e2m1fn_x4
+ACT = mybir.ActivationFunctionType
+ALU = mybir.AluOpType
+
+P = 128
+PACK = 4
+K_PASS = P * PACK
+PASSES = K // K_PASS
+GROUPS = N // K_PASS
+QUADS = 4
+BLOCK = 128
+QUARTER = 256
+HALF = 512
+RING = 512
+PER_COL = 16
+ON_VECTOR = ()
+
+
+def tile_list_blend_phase_stability_kernel(
+    tc, tab_words, tab_scales, offs, offs2, offs3, w1, w2_words, w2_scales,
+    w3_words, w3_scales, w4_words, w4_scales, b4, out_0, out_1, out_2,
+):
+    nc = tc.nc
+    with ExitStack() as ctx:
+        keep = ctx.enter_context(tc.tile_pool(name="keep", bufs=1))
+        work = ctx.enter_context(tc.tile_pool(name="work", bufs=4))
+        ypool = ctx.enter_context(tc.tile_pool(name="ypool", bufs=4))
+        psum = ctx.enter_context(tc.psum_pool(name="psum", bufs=2))
+
+        def held(shape, dtype, name):
+            return keep.tile(shape, dtype, name=name, align_bytes=64)
+
+        lists = {}
+        for name, src in (("b", offs2), ("a", offs), ("c", offs3)):
+            lists[name] = keep.tile([P, S // PER_COL], U16, name="list_" + name)
+            nc.sync.dma_start(lists[name][:], src)
+
+        tab_plane = held([P, T], U8, "tab_plane")
+        nc.vector.memset(tab_plane[:, : T // 2].bitcast(I32), 0)
+        nc.gpsimd.memset(tab_plane[:, T // 2 :].bitcast(I32), 0)
+        w_planes_raw = held([P, PASSES, K_PASS], U8, "w_planes_raw")
+        nc.gpsimd.memset(w_planes_raw[:].rearrange("p a c -> p (a c)").bitcast(I32), 0)
+        w4_planes_raw = held([P, GROUPS, K_PASS], U8, "w4_planes_raw")
+        nc.gpsimd.memset(w4_planes_raw[:].rearrange("p a c -> p (a c)").bitcast(I32), 0)
+        b_plane_1 = held([P, S], U8, "b_plane_1")
+        nc.gpsimd.memset(b_plane_1[:].bitcast(I32), 0)
+
+        tab = [held([P, T], I32, "tab%d" % a) for a in range(PASSES)]
+
+        def load_tab(a):
+            nc.sync.dma_start(out=tab[a][:], in_=tab_words[a].rearrange("p n t -> p (n t)").bitcast(I32))
+
+        for q in range(QUADS):
+            nc.sync.dma_start(
+                out=tab_plane[32 * q : 32 * q + 8, :].bitcast(I32),
+                in_=tab_scales[:, 4 * q : 4 * q + 4, :].bitcast(I32),
+            )
+        load_tab(0)
+        w1_raw = [held([P, PACK * H], F32, "w1_raw%d" % a) for a in range(PASSES)]
+        w2_raw = held([P, PASSES, H // 2], I32, "w2_raw")
+        w3_raw = held([P, PASSES, H], I32, "w3_raw")
+        w4_raw = held([P, GROUPS, K_PASS // 2], I32, "w4_raw")
+        bias = held([P, GROUPS, PACK], F32, "bias")
+
+        def load_w1(a):
+            nc.sync.dma_start(
+                out=w1_raw[a][:], in_=w1[a * K_PASS : (a + 1) * K_PASS, :].rearrange("(p j) c -> p (j c)", j=PACK)
+            )
+
+        def load_w2():
+            nc.sync.dma_start(out=w2_raw[:], in_=w2_words.rearrange("a p c -> p a c").bitcast(I32))
+
+        def load_w3():
+            nc.sync.dma_start(out=w3_raw[:], in_=w3_words.rearrange("a p c t -> p a (c t)").bitcast(I32))
+
+        def load_w4():
+            nc.sync.dma_start(out=w4_raw[:].rearrange("p g c -> p (g c)"), in_=w4_words[0].bitcast(I32))
+
+        def load_bias():
+            nc.sync.dma_start(out=bias[:], in_=b4.rearrange("(g p t) -> p g t", p=P, t=PACK))
+
+        def load_s2():
+            for q in range(QUADS):
+                nc.sync.dma_start(
+                    out=w_planes_raw[32 * q : 32 * q + 4, :, :].bitcast(I32),
+                    in_=w2_scales[:, 4 * q : 4 * q + 4, :].rearrange("a r c -> r a c").bitcast(I32),
+                )
+
+        def load_s3():
+            for q in range(QUADS):
+                nc.sync.dma_start(
+                    out=w_planes_raw[32 * q + 4 : 32 * q + 12, 0, :].bitcast(I32),
+                    in_=w3_scales[:, 4 * q : 4 * q + 4, :].bitcast(I32),
+                )
+
+        def load_s4():
+            for q in range(QUADS):
+                nc.sync.dma_start(
+                    out=w4_planes_raw[32 * q : 32 * q + 4, :, :].rearrange("p a c -> p (a c)").bitcast(I32),
+                    in_=w4_scales[0, 4 * q : 4 * q + 4, :].bitcast(I32),
+                )
+
+        planes = {}
+        for name in ("b", "a", "c"):
+            planes[name] = held([P, S], U8, "plane_" + name)
+            nc.vector.tensor_copy(planes[name][:], tab_plane[:].indirect(lists[name][:]))
+
+        def move_b():
+            for q in range(QUADS):
+                nc.sync.dma_start(
+                    out=b_plane_1[32 * q : 32 * q + 4, :].bitcast(I32),
+                    in_=planes["b"][32 * q + 4 : 32 * q + 8, :].bitcast(I32),
+                )
+
+        load_w2()
+        move_b()
+        load_w1(0)
+        load_s2()
+        load_w1(1)
+        load_w3()
+        load_s3()
+        load_tab(1)
+        load_w4()
+        load_s4()
+        load_bias()
+
+        words = {}
+
+        def gather_words(name, a, c0, width, tag):
+            piece = keep.tile([P, width], U32, name="words_%s%d_%d" % (name, a, c0), tag=tag, align_bytes=64)
+            nc.vector.tensor_copy(
+                piece[:], tab[a][:].bitcast(U32).indirect(lists[name][:, c0 // PER_COL : (c0 + width) // PER_COL])
+            )
+            for c in range(c0, c0 + width, BLOCK):
+                words[name, a, c] = piece[:, c - c0 : c - c0 + BLOCK]
+
+        for name in ("a", "b"):
+            gather_words(name, 0, 0, S, "whole_" + name)
+
+        gather_words("c", 0, 0, HALF, "half_c0")
+
+        w1_codes = held([P, PASSES, H], U32, "w1_codes")
+        w1_planes = held([P, PASSES, H], U8, "w1_planes")
+        for a in range(PASSES):
+            w1_bf = held([P, H * PACK], BF16, "w1_bf%d" % a)
+            nc.scalar.activation(
+                out=w1_bf[:].rearrange("p (t m j) -> p m j t", t=PACK, j=PACK),
+                in_=w1_raw[a][:].rearrange("p (j m t) -> p m j t", j=PACK, t=PACK),
+                func=ACT.Copy,
+            )
+            nc.vector.quantize_mx(out=w1_codes[:, a, :].bitcast(FP8X4), scales=w1_planes[:, a, :], in_=w1_bf[:])
+
+        def deal(engine_copy, raw, dtype, name):
+            dealt = held(list(raw.shape), dtype, name)
+            engine_copy(
+                out=dealt[:].rearrange("p a (t m) -> p a m t", t=PACK),
+                in_=raw.rearrange("p a (m t) -> p a m t", t=PACK),
+            )
+            return dealt
+
+        w2_codes = deal(nc.scalar.copy, w2_raw[:].bitcast(U16), U16, "w2_codes")
+        w3_codes = deal(nc.scalar.copy, w3_raw[:].bitcast(U32), U32, "w3_codes")
+        w_planes = deal(nc.vector.tensor_copy, w_planes_raw[:], U8, "w_planes")
+        w4_codes = deal(nc.scalar.copy, w4_raw[:].bitcast(U16), U16, "w4_codes")
+
+
+        w4_planes = deal(nc.vector.tensor_copy, w4_planes_raw[:], U8, "w4_planes")
+
+        def first_product(name, c):
+            bank = psum.tile([P, PACK, BLOCK], F32, name="bank_" + name, tag="c" if name == "c" else "aby", bufs=2 if name == "c" else 6)
+            cols = slice(c, c + BLOCK)
+            for t in range(PACK):
+                tcols = slice(t * P, (t + 1) * P)
+                for a in range(PASSES):
+                    if name == "a":
+                        lhs, lhs_scale = w1_codes[:, a, tcols].bitcast(FP8X4), w1_planes[:, a, tcols]
+                        rhs_scale = planes["a"][4 * a :, cols]
+                    elif name == "b":
+                        lhs, lhs_scale = w2_codes[:, a, tcols].bitcast(FP4X4), w_planes[:, a, tcols]
+                        rhs_scale = (planes["b"], b_plane_1)[a][:, cols]
+                    else:
+                        lhs, lhs_scale = w3_codes[:, a, tcols].bitcast(FP8X4), w_planes[4 + 4 * a :, 0, tcols]
+                        rhs_scale = planes["c"][4 * a :, cols]
+                    nc.tensor.matmul_mx(
+                        out=bank[:, t, :], lhsT=lhs, lhsT_scale=lhs_scale,
+                        rhs=words[name, a, c].bitcast(FP8X4), rhs_scale=rhs_scale,
+                        start=(a == 0), stop=(a == PASSES - 1),
+                    )
+            return bank[:].rearrange("p t j -> p j t")
+
+        mags = {}
+
+        def magnitudes(c0, width):
+            if c0 % QUARTER == 0:
+                for name in ("a", "b"):
+                    gather_words(name, 1, c0, QUARTER, "quarter_%s%d" % (name, c0 % RING))
+            for name in ("a", "b"):
+                mags[name, c0] = work.tile([P, width * PACK], F32, name="mag_" + name)
+            for c in range(c0, c0 + width, BLOCK):
+                for name in ("a", "b"):
+                    o = (c - c0) * PACK
+                    nc.scalar.activation(
+                        out=mags[name, c0][:, o : o + BLOCK * PACK].rearrange("p (j t) -> p j t", t=PACK),
+                        in_=first_product(name, c), func=ACT.Abs,
+                    )
+
+        y_codes = held([P, GROUPS, S], U32, "y_codes")
+        y_planes = held([P, GROUPS, S], U8, "y_planes")
+        ys = {}
+        hq = {}
+
+        def latent(c0, width):
+            if c0 == 0:
+                gather_words("c", 1, 0, HALF, "half_c1")
+            if c0 == HALF:
+                gather_words("c", 0, HALF, HALF, "half_c0")
+                gather_words("c", 1, HALF, HALF, "half_c1")
+            root = mags["a", c0]
+            nc.vector.tensor_tensor(out=root[:], in0=root[:], in1=mags["b", c0][:], op=ALU.mult)
+            nc.scalar.activation(out=root[:], in_=root[:], func=ACT.Sqrt)
+            h_bf = work.tile([P, width * PACK], BF16, name="h_bf", align_bytes=64)
+            for c in range(c0, c0 + width, BLOCK):
+                o = (c - c0) * PACK
+                nc.vector.tensor_tensor(
+                    out=h_bf[:, o : o + BLOCK * PACK].rearrange("p (j t) -> p j t", t=PACK),
+                    in0=root[:, o : o + BLOCK * PACK].rearrange("p (j t) -> p j t", t=PACK),
+                    in1=first_product("c", c), op=ALU.subtract,
+                )
+            h_codes = work.tile([P, width], U32, name="h_codes", align_bytes=64)
+            h_plane = work.tile([P, width], U8, name="h_plane", align_bytes=64)
+            nc.vector.quantize_mx(out=h_codes[:].bitcast(FP8X4), scales=h_plane[:], in_=h_bf[:])
+            hq[c0] = (h_codes, h_plane)
+
+        def scores(c0, width):
+            h_codes, h_plane = hq[c0]
+            for g in range(GROUPS):
+                y = ypool.tile([P, PACK, width], F32, name="y%d" % g)
+                ys[g, c0] = y
+                for u in range(2):
+                    bank = psum.tile([P, 2, width], F32, name="bank_y", tag="aby", bufs=6)
+                    for e in range(2):
+                        t = 2 * u + e
+                        tcols = slice(t * P, (t + 1) * P)
+                        nc.tensor.matmul_mx(
+                            out=bank[:, e, :], lhsT=w4_codes[:, g, tcols].bitcast(FP4X4),
+                            lhsT_scale=w4_planes[:, g, tcols],
+                            rhs=h_codes[:].bitcast(FP8X4), rhs_scale=h_plane[:], start=True, stop=True,
+                        )
+                    for e in range(2):
+                        t = 2 * u + e
+                        if (c0, g, u) in ON_VECTOR:
+                            nc.vector.tensor_scalar(
+                                out=y[:, t, :], in0=bank[:, e, :], scalar1=bias[:, g, t : t + 1], scalar2=None, op0=ALU.add
+                            )
+                        else:
+                            nc.scalar.activation(
+                                out=y[:, t, :], in_=bank[:, e, :], func=ACT.Identity, bias=bias[:, g, t : t + 1]
+                            )
+                nc.sync.dma_start(
+                    out=out_0[g * K_PASS : (g + 1) * K_PASS, c0 : c0 + width].rearrange("(p t) j -> p t j", t=PACK),
+                    in_=y[:],
+                )
+
+        def planes_out(c0, width):
+            cols = slice(c0, c0 + width)
+            y_bf = {}
+            for g in range(GROUPS):
+                y_bf[g] = work.tile([P, width * PACK], BF16, name="y_bf%d" % g, align_bytes=64)
+                nc.vector.tensor_copy(
+                    out=y_bf[g][:].rearrange("p (c i t) -> p c t i", i=PACK, t=PACK),
+                    in_=ys[g, c0][:].rearrange("p t (c i) -> p c t i", i=PACK),
+                )
+            for g in range(GROUPS):
+                nc.vector.quantize_mx(
+                    out=y_codes[:, g, cols].bitcast(FP8X4), scales=y_planes[:, g, cols], in_=y_bf[g][:]
+                )
+
+        def words_out(c0, width):
+            cols = slice(c0, c0 + width)
+            (nc.scalar if c0 + width == S else nc.sync).dma_start(
+                out=out_1.rearrange("g p m t -> p g (m t)")[:, :, PACK * c0 : PACK * (c0 + width)].bitcast(I32),
+                in_=y_codes[:, :, cols].bitcast(I32),
+            )
+
+        magnitudes(0, 256)
+        magnitudes(256, 256)
+        latent(0, 256)
+        magnitudes(512, 256)
+        latent(256, 256)
+        scores(0, 256)
+        magnitudes(768, 256)
+        latent(512, 256)
+        scores(256, 256)
+        latent(768, 256)
+        planes_out(0, 256)
+        words_out(0, 256)
+        scores(512, 256)
+        planes_out(256, 256)
+        words_out(256, 256)
+        scores(768, 256)
+        planes_out(512, 256)
+        words_out(512, 256)
+        planes_out(768, 256)
+        words_out(768, 256)
+        for q in range(QUADS):
+            nc.scalar.dma_start(
+                out=out_2[:, 4 * q : 4 * q + 4, :].rearrange("g r c -> r g c").bitcast(I32),
+                in_=y_planes[32 * q : 32 * q + 4, :, :].bitcast(I32),
+            )

@@ -25,9 +25,11 @@ QUADS = 4
 BLOCK = 128
 QUARTER = 256
 HALF = 512
+NB = 4
 RING = 512
 PER_COL = 16
-ON_VECTOR = ()
+ON_VECTOR = ((768,1,1),)
+ON_SCALAR = ()
 
 
 def tile_list_blend_phase_stability_kernel(
@@ -50,21 +52,20 @@ def tile_list_blend_phase_stability_kernel(
             nc.sync.dma_start(lists[name][:], src)
 
         tab_plane = held([P, T], U8, "tab_plane")
-        nc.vector.memset(tab_plane[:, : T // 2].bitcast(I32), 0)
-        nc.gpsimd.memset(tab_plane[:, T // 2 :].bitcast(I32), 0)
+        nc.vector.memset(tab_plane[:].bitcast(I32), 0)
         w_planes_raw = held([P, PASSES, K_PASS], U8, "w_planes_raw")
-        nc.gpsimd.memset(w_planes_raw[:].rearrange("p a c -> p (a c)").bitcast(I32), 0)
+        nc.vector.memset(w_planes_raw[:].rearrange("p a c -> p (a c)").bitcast(I32), 0)
         w4_planes_raw = held([P, GROUPS, K_PASS], U8, "w4_planes_raw")
-        nc.gpsimd.memset(w4_planes_raw[:].rearrange("p a c -> p (a c)").bitcast(I32), 0)
+        nc.vector.memset(w4_planes_raw[:].rearrange("p a c -> p (a c)").bitcast(I32), 0)
         b_plane_1 = held([P, S], U8, "b_plane_1")
-        nc.gpsimd.memset(b_plane_1[:].bitcast(I32), 0)
+        nc.vector.memset(b_plane_1[:].bitcast(I32), 0)
 
         tab = [held([P, T], I32, "tab%d" % a) for a in range(PASSES)]
 
         def load_tab(a):
             nc.sync.dma_start(out=tab[a][:], in_=tab_words[a].rearrange("p n t -> p (n t)").bitcast(I32))
 
-        for q in range(QUADS):
+        for q in (0, 2, 1, 3):
             nc.sync.dma_start(
                 out=tab_plane[32 * q : 32 * q + 8, :].bitcast(I32),
                 in_=tab_scales[:, 4 * q : 4 * q + 4, :].bitcast(I32),
@@ -94,24 +95,24 @@ def tile_list_blend_phase_stability_kernel(
             nc.sync.dma_start(out=bias[:], in_=b4.rearrange("(g p t) -> p g t", p=P, t=PACK))
 
         def load_s2():
-            for q in range(QUADS):
+            for r in range(4):
                 nc.sync.dma_start(
-                    out=w_planes_raw[32 * q : 32 * q + 4, :, :].bitcast(I32),
-                    in_=w2_scales[:, 4 * q : 4 * q + 4, :].rearrange("a r c -> r a c").bitcast(I32),
+                    out=w_planes_raw[r:P:32, :, :].bitcast(I32),
+                    in_=w2_scales[:, r:16:4, :].rearrange("a q c -> q a c").bitcast(I32),
                 )
 
         def load_s3():
-            for q in range(QUADS):
+            for q in (0, 2, 1, 3):
                 nc.sync.dma_start(
                     out=w_planes_raw[32 * q + 4 : 32 * q + 12, 0, :].bitcast(I32),
                     in_=w3_scales[:, 4 * q : 4 * q + 4, :].bitcast(I32),
                 )
 
         def load_s4():
-            for q in range(QUADS):
+            for r in range(4):
                 nc.sync.dma_start(
-                    out=w4_planes_raw[32 * q : 32 * q + 4, :, :].rearrange("p a c -> p (a c)").bitcast(I32),
-                    in_=w4_scales[0, 4 * q : 4 * q + 4, :].bitcast(I32),
+                    out=w4_planes_raw[r:P:32, :, :].rearrange("p a c -> p (a c)").bitcast(I32),
+                    in_=w4_scales[0, r:16:4, :].bitcast(I32),
                 )
 
         planes = {}
@@ -120,10 +121,10 @@ def tile_list_blend_phase_stability_kernel(
             nc.vector.tensor_copy(planes[name][:], tab_plane[:].indirect(lists[name][:]))
 
         def move_b():
-            for q in range(QUADS):
+            for r in range(4):
                 nc.sync.dma_start(
-                    out=b_plane_1[32 * q : 32 * q + 4, :].bitcast(I32),
-                    in_=planes["b"][32 * q + 4 : 32 * q + 8, :].bitcast(I32),
+                    out=b_plane_1[r:P:32, :].bitcast(I32),
+                    in_=planes["b"][4 + r : P : 32, :].bitcast(I32),
                 )
 
         load_w2()
@@ -167,8 +168,8 @@ def tile_list_blend_phase_stability_kernel(
         def deal(engine_copy, raw, dtype, name):
             dealt = held(list(raw.shape), dtype, name)
             engine_copy(
-                out=dealt[:].rearrange("p a (t m) -> p a m t", t=PACK),
-                in_=raw.rearrange("p a (m t) -> p a m t", t=PACK),
+                out=dealt[:].rearrange("p a (t m) -> p a t m", t=PACK),
+                in_=raw.rearrange("p a (m t) -> p a t m", t=PACK),
             )
             return dealt
 
@@ -204,19 +205,16 @@ def tile_list_blend_phase_stability_kernel(
 
         mags = {}
 
-        def magnitudes(c0, width):
+        def magnitudes(name, c0, width):
             if c0 % QUARTER == 0:
-                for name in ("a", "b"):
-                    gather_words(name, 1, c0, QUARTER, "quarter_%s%d" % (name, c0 % RING))
-            for name in ("a", "b"):
-                mags[name, c0] = work.tile([P, width * PACK], F32, name="mag_" + name)
+                gather_words(name, 1, c0, QUARTER, "quarter_%s%d" % (name, c0 % RING))
+            mags[name, c0] = work.tile([P, width * PACK], F32, name="mag_" + name)
             for c in range(c0, c0 + width, BLOCK):
-                for name in ("a", "b"):
-                    o = (c - c0) * PACK
-                    nc.scalar.activation(
-                        out=mags[name, c0][:, o : o + BLOCK * PACK].rearrange("p (j t) -> p j t", t=PACK),
-                        in_=first_product(name, c), func=ACT.Abs,
-                    )
+                o = (c - c0) * PACK
+                nc.scalar.activation(
+                    out=mags[name, c0][:, o : o + BLOCK * PACK].rearrange("p (j t) -> p j t", t=PACK),
+                    in_=first_product(name, c), func=ACT.Abs,
+                )
 
         y_codes = held([P, GROUPS, S], U32, "y_codes")
         y_planes = held([P, GROUPS, S], U8, "y_planes")
@@ -232,7 +230,7 @@ def tile_list_blend_phase_stability_kernel(
             root = mags["a", c0]
             nc.vector.tensor_tensor(out=root[:], in0=root[:], in1=mags["b", c0][:], op=ALU.mult)
             nc.scalar.activation(out=root[:], in_=root[:], func=ACT.Sqrt)
-            h_bf = work.tile([P, width * PACK], BF16, name="h_bf", align_bytes=64)
+            h_bf = work.tile([P, width * PACK], BF16, name="h_bf", tag="rounded", bufs=NB, align_bytes=64)
             for c in range(c0, c0 + width, BLOCK):
                 o = (c - c0) * PACK
                 nc.vector.tensor_tensor(
@@ -279,8 +277,8 @@ def tile_list_blend_phase_stability_kernel(
             cols = slice(c0, c0 + width)
             y_bf = {}
             for g in range(GROUPS):
-                y_bf[g] = work.tile([P, width * PACK], BF16, name="y_bf%d" % g, align_bytes=64)
-                nc.vector.tensor_copy(
+                y_bf[g] = work.tile([P, width * PACK], BF16, name="y_bf%d" % g, tag="rounded", bufs=NB, align_bytes=64)
+                (nc.scalar.copy if (c0, g) in ON_SCALAR else nc.vector.tensor_copy)(
                     out=y_bf[g][:].rearrange("p (c i t) -> p c t i", i=PACK, t=PACK),
                     in_=ys[g, c0][:].rearrange("p t (c i) -> p c t i", i=PACK),
                 )
@@ -291,18 +289,29 @@ def tile_list_blend_phase_stability_kernel(
 
         def words_out(c0, width):
             cols = slice(c0, c0 + width)
-            (nc.scalar if c0 + width == S else nc.sync).dma_start(
-                out=out_1.rearrange("g p m t -> p g (m t)")[:, :, PACK * c0 : PACK * (c0 + width)].bitcast(I32),
-                in_=y_codes[:, :, cols].bitcast(I32),
-            )
+            if c0 + width < S:
+                nc.sync.dma_start(
+                    out=out_1.rearrange("g p m t -> p g (m t)")[:, :, PACK * c0 : PACK * (c0 + width)].bitcast(I32),
+                    in_=y_codes[:, :, cols].bitcast(I32),
+                )
+            else:
+                for g in range(GROUPS):
+                    nc.scalar.dma_start(
+                        out=out_1[g].rearrange("p m t -> p (m t)")[:, PACK * c0 : PACK * (c0 + width)].bitcast(I32),
+                        in_=y_codes[:, g, cols].bitcast(I32),
+                    )
 
-        magnitudes(0, 256)
-        magnitudes(256, 256)
+        magnitudes("a", 0, 256)
+        magnitudes("b", 0, 256)
+        magnitudes("a", 256, 256)
+        magnitudes("b", 256, 256)
         latent(0, 256)
-        magnitudes(512, 256)
+        magnitudes("a", 512, 256)
+        magnitudes("b", 512, 256)
         latent(256, 256)
         scores(0, 256)
-        magnitudes(768, 256)
+        magnitudes("a", 768, 256)
+        magnitudes("b", 768, 256)
         latent(512, 256)
         scores(256, 256)
         latent(768, 256)
@@ -316,8 +325,8 @@ def tile_list_blend_phase_stability_kernel(
         words_out(512, 256)
         planes_out(768, 256)
         words_out(768, 256)
-        for q in range(QUADS):
+        for r in range(4):
             nc.scalar.dma_start(
-                out=out_2[:, 4 * q : 4 * q + 4, :].rearrange("g r c -> r g c").bitcast(I32),
-                in_=y_planes[32 * q : 32 * q + 4, :, :].bitcast(I32),
+                out=out_2[:, r:16:4, :].rearrange("g q c -> q g c").bitcast(I32),
+                in_=y_planes[r:P:32, :, :].bitcast(I32),
             )

@@ -28,7 +28,7 @@ HALF = 512
 NB = 4
 RING = 512
 PER_COL = 16
-ON_VECTOR = ((768,1,1),)
+ON_VECTOR = ()
 ON_SCALAR = ()
 
 
@@ -152,7 +152,7 @@ def tile_list_blend_phase_stability_kernel(
         for name in ("a", "b"):
             gather_words(name, 0, 0, S, "whole_" + name)
 
-        gather_words("c", 0, 0, HALF, "half_c0")
+        gather_words("c", 0, 0, S, "whole_c")
 
         w1_codes = held([P, PASSES, H], U32, "w1_codes")
         w1_planes = held([P, PASSES, H], U8, "w1_planes")
@@ -175,11 +175,11 @@ def tile_list_blend_phase_stability_kernel(
 
         w2_codes = deal(nc.scalar.copy, w2_raw[:].bitcast(U16), U16, "w2_codes")
         w3_codes = deal(nc.scalar.copy, w3_raw[:].bitcast(U32), U32, "w3_codes")
-        w_planes = deal(nc.vector.tensor_copy, w_planes_raw[:], U8, "w_planes")
+        w_planes = deal(nc.gpsimd.tensor_copy, w_planes_raw[:], U8, "w_planes")
         w4_codes = deal(nc.scalar.copy, w4_raw[:].bitcast(U16), U16, "w4_codes")
 
 
-        w4_planes = deal(nc.vector.tensor_copy, w4_planes_raw[:], U8, "w4_planes")
+        w4_planes = deal(nc.gpsimd.tensor_copy, w4_planes_raw[:], U8, "w4_planes")
 
         def first_product(name, c):
             bank = psum.tile([P, PACK, BLOCK], F32, name="bank_" + name, tag="c" if name == "c" else "aby", bufs=2 if name == "c" else 6)
@@ -225,7 +225,6 @@ def tile_list_blend_phase_stability_kernel(
             if c0 == 0:
                 gather_words("c", 1, 0, HALF, "half_c1")
             if c0 == HALF:
-                gather_words("c", 0, HALF, HALF, "half_c0")
                 gather_words("c", 1, HALF, HALF, "half_c1")
             root = mags["a", c0]
             nc.vector.tensor_tensor(out=root[:], in0=root[:], in1=mags["b", c0][:], op=ALU.mult)
@@ -289,17 +288,10 @@ def tile_list_blend_phase_stability_kernel(
 
         def words_out(c0, width):
             cols = slice(c0, c0 + width)
-            if c0 + width < S:
-                nc.sync.dma_start(
-                    out=out_1.rearrange("g p m t -> p g (m t)")[:, :, PACK * c0 : PACK * (c0 + width)].bitcast(I32),
-                    in_=y_codes[:, :, cols].bitcast(I32),
-                )
-            else:
-                for g in range(GROUPS):
-                    nc.scalar.dma_start(
-                        out=out_1[g].rearrange("p m t -> p (m t)")[:, PACK * c0 : PACK * (c0 + width)].bitcast(I32),
-                        in_=y_codes[:, g, cols].bitcast(I32),
-                    )
+            (nc.scalar if c0 + width == S else nc.sync).dma_start(
+                out=out_1.rearrange("g p m t -> p g (m t)")[:, :, PACK * c0 : PACK * (c0 + width)].bitcast(I32),
+                in_=y_codes[:, :, cols].bitcast(I32),
+            )
 
         magnitudes("a", 0, 256)
         magnitudes("b", 0, 256)
@@ -314,9 +306,9 @@ def tile_list_blend_phase_stability_kernel(
         magnitudes("b", 768, 256)
         latent(512, 256)
         scores(256, 256)
-        latent(768, 256)
         planes_out(0, 256)
         words_out(0, 256)
+        latent(768, 256)
         scores(512, 256)
         planes_out(256, 256)
         words_out(256, 256)

@@ -21,15 +21,18 @@ PACK = 4
 K_PASS = P * PACK
 PASSES = K // K_PASS
 GROUPS = N // K_PASS
-QUADS = 4
+QUAD = 32
+QUAD_ROWS = 4
+SCALE_ROWS = 16
+QUAD_ORDER = (0, 2, 1, 3)
+ENTRIES_PER_COLUMN = 16
 BLOCK = 128
-QUARTER = 256
-HALF = 512
-NB = 4
-RING = 512
-PER_COL = 16
-ON_VECTOR = ()
-ON_SCALAR = ()
+CHUNK = 256
+CHUNKS = S // CHUNK
+HALF = S // 2
+SHARED_BANKS = 6
+C_BANKS = 2
+ROUNDED_TILES = 4
 
 
 def tile_list_blend_phase_stability_kernel(
@@ -39,135 +42,106 @@ def tile_list_blend_phase_stability_kernel(
     nc = tc.nc
     with ExitStack() as ctx:
         keep = ctx.enter_context(tc.tile_pool(name="keep", bufs=1))
-        work = ctx.enter_context(tc.tile_pool(name="work", bufs=4))
-        ypool = ctx.enter_context(tc.tile_pool(name="ypool", bufs=4))
-        psum = ctx.enter_context(tc.psum_pool(name="psum", bufs=2))
+        work = ctx.enter_context(tc.tile_pool(name="work", bufs=CHUNKS))
+        psum = ctx.enter_context(tc.psum_pool(name="psum", bufs=1))
 
-        def held(shape, dtype, name):
-            return keep.tile(shape, dtype, name=name, align_bytes=64)
+        def held(shape, dtype, name, tag=None):
+            return keep.tile(shape, dtype, name=name, tag=tag or name, align_bytes=64)
 
         lists = {}
-        for name, src in (("b", offs2), ("a", offs), ("c", offs3)):
-            lists[name] = keep.tile([P, S // PER_COL], U16, name="list_" + name)
-            nc.sync.dma_start(lists[name][:], src)
+        for name, source in (("b", offs2), ("a", offs), ("c", offs3)):
+            lists[name] = keep.tile([P, S // ENTRIES_PER_COLUMN], U16, name="list_" + name)
+            nc.sync.dma_start(lists[name][:], source)
 
         tab_plane = held([P, T], U8, "tab_plane")
         nc.vector.memset(tab_plane[:].bitcast(I32), 0)
-        w_planes_raw = held([P, PASSES, K_PASS], U8, "w_planes_raw")
-        nc.vector.memset(w_planes_raw[:].rearrange("p a c -> p (a c)").bitcast(I32), 0)
+        w23_planes_raw = held([P, PASSES, H], U8, "w23_planes_raw", tag="c_words_0")
+        nc.vector.memset(w23_planes_raw[:].rearrange("p a c -> p (a c)").bitcast(I32), 0)
         w4_planes_raw = held([P, GROUPS, K_PASS], U8, "w4_planes_raw")
-        nc.vector.memset(w4_planes_raw[:].rearrange("p a c -> p (a c)").bitcast(I32), 0)
+        nc.vector.memset(w4_planes_raw[:].rearrange("p g c -> p (g c)").bitcast(I32), 0)
         b_plane_1 = held([P, S], U8, "b_plane_1")
         nc.vector.memset(b_plane_1[:].bitcast(I32), 0)
 
         tab = [held([P, T], I32, "tab%d" % a) for a in range(PASSES)]
-
-        def load_tab(a):
-            nc.sync.dma_start(out=tab[a][:], in_=tab_words[a].rearrange("p n t -> p (n t)").bitcast(I32))
-
-        for q in (0, 2, 1, 3):
-            nc.sync.dma_start(
-                out=tab_plane[32 * q : 32 * q + 8, :].bitcast(I32),
-                in_=tab_scales[:, 4 * q : 4 * q + 4, :].bitcast(I32),
-            )
-        load_tab(0)
         w1_raw = [held([P, PACK * H], F32, "w1_raw%d" % a) for a in range(PASSES)]
         w2_raw = held([P, PASSES, H // 2], I32, "w2_raw")
         w3_raw = held([P, PASSES, H], I32, "w3_raw")
         w4_raw = held([P, GROUPS, K_PASS // 2], I32, "w4_raw")
         bias = held([P, GROUPS, PACK], F32, "bias")
 
+        def load_tab(a):
+            nc.sync.dma_start(out=tab[a][:], in_=tab_words[a].rearrange("p n i -> p (n i)").bitcast(I32))
+
         def load_w1(a):
-            nc.sync.dma_start(
-                out=w1_raw[a][:], in_=w1[a * K_PASS : (a + 1) * K_PASS, :].rearrange("(p j) c -> p (j c)", j=PACK)
-            )
+            rows = w1[a * K_PASS : (a + 1) * K_PASS, :]
+            nc.sync.dma_start(out=w1_raw[a][:], in_=rows.rearrange("(p i) c -> p (i c)", i=PACK))
 
-        def load_w2():
-            nc.sync.dma_start(out=w2_raw[:], in_=w2_words.rearrange("a p c -> p a c").bitcast(I32))
-
-        def load_w3():
-            nc.sync.dma_start(out=w3_raw[:], in_=w3_words.rearrange("a p c t -> p a (c t)").bitcast(I32))
-
-        def load_w4():
-            nc.sync.dma_start(out=w4_raw[:].rearrange("p g c -> p (g c)"), in_=w4_words[0].bitcast(I32))
-
-        def load_bias():
-            nc.sync.dma_start(out=bias[:], in_=b4.rearrange("(g p t) -> p g t", p=P, t=PACK))
-
-        def load_s2():
-            for r in range(4):
+        def load_both_passes(plane, first, scales):
+            for quad in QUAD_ORDER:
+                start = QUAD * quad + first
                 nc.sync.dma_start(
-                    out=w_planes_raw[r:P:32, :, :].bitcast(I32),
-                    in_=w2_scales[:, r:16:4, :].rearrange("a q c -> q a c").bitcast(I32),
+                    out=plane[start : start + PASSES * QUAD_ROWS, :].bitcast(I32),
+                    in_=scales[:, QUAD_ROWS * quad : QUAD_ROWS * (quad + 1), :].bitcast(I32),
                 )
 
-        def load_s3():
-            for q in (0, 2, 1, 3):
-                nc.sync.dma_start(
-                    out=w_planes_raw[32 * q + 4 : 32 * q + 12, 0, :].bitcast(I32),
-                    in_=w3_scales[:, 4 * q : 4 * q + 4, :].bitcast(I32),
-                )
-
-        def load_s4():
-            for r in range(4):
-                nc.sync.dma_start(
-                    out=w4_planes_raw[r:P:32, :, :].rearrange("p a c -> p (a c)").bitcast(I32),
-                    in_=w4_scales[0, r:16:4, :].bitcast(I32),
-                )
+        nc.sync.dma_start(out=w2_raw[:], in_=w2_words.rearrange("a p c -> p a c").bitcast(I32))
+        load_both_passes(tab_plane, 0, tab_scales)
+        load_tab(0)
 
         planes = {}
         for name in ("b", "a", "c"):
             planes[name] = held([P, S], U8, "plane_" + name)
             nc.vector.tensor_copy(planes[name][:], tab_plane[:].indirect(lists[name][:]))
 
-        def move_b():
-            for r in range(4):
-                nc.sync.dma_start(
-                    out=b_plane_1[r:P:32, :].bitcast(I32),
-                    in_=planes["b"][4 + r : P : 32, :].bitcast(I32),
-                )
-
-        load_w2()
-        move_b()
+        for r in range(QUAD_ROWS):
+            nc.sync.dma_start(
+                out=b_plane_1[r:P:QUAD, :].bitcast(I32),
+                in_=planes["b"][QUAD_ROWS + r : P : QUAD, :].bitcast(I32),
+            )
         load_w1(0)
-        load_s2()
+        for r in range(QUAD_ROWS):
+            nc.sync.dma_start(
+                out=w23_planes_raw[r:P:QUAD, :, :].bitcast(I32),
+                in_=w2_scales[:, r:SCALE_ROWS:QUAD_ROWS, :].rearrange("a q c -> q a c").bitcast(I32),
+            )
         load_w1(1)
-        load_w3()
-        load_s3()
+        load_both_passes(w23_planes_raw[:, 0, :], QUAD_ROWS, w3_scales)
+        nc.sync.dma_start(out=w3_raw[:], in_=w3_words.rearrange("a p c i -> p a (c i)").bitcast(I32))
+        nc.sync.dma_start(out=w4_raw[:].rearrange("p g c -> p (g c)"), in_=w4_words[0].bitcast(I32))
         load_tab(1)
-        load_w4()
-        load_s4()
-        load_bias()
+        for r in range(QUAD_ROWS):
+            nc.sync.dma_start(
+                out=w4_planes_raw[r:P:QUAD, :, :].rearrange("p g c -> p (g c)").bitcast(I32),
+                in_=w4_scales[0, r:SCALE_ROWS:QUAD_ROWS, :].bitcast(I32),
+            )
+        nc.sync.dma_start(out=bias[:], in_=b4.rearrange("(g p t) -> p g t", p=P, t=PACK))
 
         words = {}
 
         def gather_words(name, a, c0, width, tag):
-            piece = keep.tile([P, width], U32, name="words_%s%d_%d" % (name, a, c0), tag=tag, align_bytes=64)
-            nc.vector.tensor_copy(
-                piece[:], tab[a][:].bitcast(U32).indirect(lists[name][:, c0 // PER_COL : (c0 + width) // PER_COL])
-            )
+            piece = held([P, width], U32, "words_%s%d_%d" % (name, a, c0), tag=tag)
+            entries = lists[name][:, c0 // ENTRIES_PER_COLUMN : (c0 + width) // ENTRIES_PER_COLUMN]
+            nc.vector.tensor_copy(piece[:], tab[a][:].bitcast(U32).indirect(entries))
             for c in range(c0, c0 + width, BLOCK):
                 words[name, a, c] = piece[:, c - c0 : c - c0 + BLOCK]
 
         for name in ("a", "b"):
-            gather_words(name, 0, 0, S, "whole_" + name)
-
-        gather_words("c", 0, 0, S, "whole_c")
+            gather_words(name, 0, 0, S, name + "_words_0")
 
         w1_codes = held([P, PASSES, H], U32, "w1_codes")
         w1_planes = held([P, PASSES, H], U8, "w1_planes")
         for a in range(PASSES):
             w1_bf = held([P, H * PACK], BF16, "w1_bf%d" % a)
             nc.scalar.activation(
-                out=w1_bf[:].rearrange("p (t m j) -> p m j t", t=PACK, j=PACK),
-                in_=w1_raw[a][:].rearrange("p (j m t) -> p m j t", j=PACK, t=PACK),
+                out=w1_bf[:].rearrange("p (t m i) -> p m i t", t=PACK, i=PACK),
+                in_=w1_raw[a][:].rearrange("p (i m t) -> p m i t", i=PACK, t=PACK),
                 func=ACT.Copy,
             )
             nc.vector.quantize_mx(out=w1_codes[:, a, :].bitcast(FP8X4), scales=w1_planes[:, a, :], in_=w1_bf[:])
 
-        def deal(engine_copy, raw, dtype, name):
+        def deal(copy, raw, dtype, name):
             dealt = held(list(raw.shape), dtype, name)
-            engine_copy(
+            copy(
                 out=dealt[:].rearrange("p a (t m) -> p a t m", t=PACK),
                 in_=raw.rearrange("p a (m t) -> p a t m", t=PACK),
             )
@@ -175,150 +149,131 @@ def tile_list_blend_phase_stability_kernel(
 
         w2_codes = deal(nc.scalar.copy, w2_raw[:].bitcast(U16), U16, "w2_codes")
         w3_codes = deal(nc.scalar.copy, w3_raw[:].bitcast(U32), U32, "w3_codes")
-        w_planes = deal(nc.gpsimd.tensor_copy, w_planes_raw[:], U8, "w_planes")
+        w23_planes = deal(nc.vector.tensor_copy, w23_planes_raw[:], U8, "w23_planes")
+        gather_words("c", 0, 0, HALF, "c_words_0")
         w4_codes = deal(nc.scalar.copy, w4_raw[:].bitcast(U16), U16, "w4_codes")
-
-
-        w4_planes = deal(nc.gpsimd.tensor_copy, w4_planes_raw[:], U8, "w4_planes")
+        w4_planes = deal(nc.vector.tensor_copy, w4_planes_raw[:], U8, "w4_planes")
 
         def first_product(name, c):
-            bank = psum.tile([P, PACK, BLOCK], F32, name="bank_" + name, tag="c" if name == "c" else "aby", bufs=2 if name == "c" else 6)
+            if name == "c":
+                bank = psum.tile([P, PACK, BLOCK], F32, name="bank_c", tag="c", bufs=C_BANKS)
+            else:
+                bank = psum.tile([P, PACK, BLOCK], F32, name="bank_" + name, tag="shared", bufs=SHARED_BANKS)
             cols = slice(c, c + BLOCK)
-            for t in range(PACK):
-                tcols = slice(t * P, (t + 1) * P)
-                for a in range(PASSES):
+            for a in range(PASSES):
+                for t in range(PACK):
+                    slice_t = slice(t * P, (t + 1) * P)
                     if name == "a":
-                        lhs, lhs_scale = w1_codes[:, a, tcols].bitcast(FP8X4), w1_planes[:, a, tcols]
-                        rhs_scale = planes["a"][4 * a :, cols]
+                        lhs, lhs_scale = w1_codes[:, a, slice_t].bitcast(FP8X4), w1_planes[:, a, slice_t]
+                        rhs_scale = planes["a"][QUAD_ROWS * a :, cols]
                     elif name == "b":
-                        lhs, lhs_scale = w2_codes[:, a, tcols].bitcast(FP4X4), w_planes[:, a, tcols]
+                        lhs, lhs_scale = w2_codes[:, a, slice_t].bitcast(FP4X4), w23_planes[:, a, slice_t]
                         rhs_scale = (planes["b"], b_plane_1)[a][:, cols]
                     else:
-                        lhs, lhs_scale = w3_codes[:, a, tcols].bitcast(FP8X4), w_planes[4 + 4 * a :, 0, tcols]
-                        rhs_scale = planes["c"][4 * a :, cols]
+                        lhs = w3_codes[:, a, slice_t].bitcast(FP8X4)
+                        lhs_scale = w23_planes[QUAD_ROWS * (a + 1) :, 0, slice_t]
+                        rhs_scale = planes["c"][QUAD_ROWS * a :, cols]
                     nc.tensor.matmul_mx(
                         out=bank[:, t, :], lhsT=lhs, lhsT_scale=lhs_scale,
                         rhs=words[name, a, c].bitcast(FP8X4), rhs_scale=rhs_scale,
-                        start=(a == 0), stop=(a == PASSES - 1),
+                        start=(a == 0 and t == 0), stop=(a == PASSES - 1 and t == PACK - 1),
                     )
             return bank[:].rearrange("p t j -> p j t")
 
-        mags = {}
+        def block_of(tile, c0, c):
+            start = (c - c0) * PACK
+            return tile[:, start : start + BLOCK * PACK].rearrange("p (j t) -> p j t", t=PACK)
 
-        def magnitudes(name, c0, width):
-            if c0 % QUARTER == 0:
-                gather_words(name, 1, c0, QUARTER, "quarter_%s%d" % (name, c0 % RING))
-            mags[name, c0] = work.tile([P, width * PACK], F32, name="mag_" + name)
-            for c in range(c0, c0 + width, BLOCK):
-                o = (c - c0) * PACK
-                nc.scalar.activation(
-                    out=mags[name, c0][:, o : o + BLOCK * PACK].rearrange("p (j t) -> p j t", t=PACK),
-                    in_=first_product(name, c), func=ACT.Abs,
-                )
-
+        mags, h_quantised, scores_f32 = {}, {}, {}
         y_codes = held([P, GROUPS, S], U32, "y_codes")
         y_planes = held([P, GROUPS, S], U8, "y_planes")
-        ys = {}
-        hq = {}
 
-        def latent(c0, width):
+        def magnitudes(i):
+            c0 = i * CHUNK
+            for name in ("a", "b"):
+                if c0 < HALF:
+                    tag = "%s_words_1_%d" % (name, i)
+                elif name == "a":
+                    tag = "mag_b%d" % (i - 2)
+                else:
+                    tag = "b_words_1_%d" % (i - 1)
+                gather_words(name, 1, c0, CHUNK, tag)
+                mags[name, i] = held([P, CHUNK * PACK], F32, "mag_%s%d" % (name, i))
+                for c in range(c0, c0 + CHUNK, BLOCK):
+                    nc.scalar.activation(out=block_of(mags[name, i], c0, c), in_=first_product(name, c), func=ACT.Abs)
+
+        def latent(i):
+            c0 = i * CHUNK
             if c0 == 0:
-                gather_words("c", 1, 0, HALF, "half_c1")
+                gather_words("c", 1, c0, HALF, "c_words_1")
             if c0 == HALF:
-                gather_words("c", 1, HALF, HALF, "half_c1")
-            root = mags["a", c0]
-            nc.vector.tensor_tensor(out=root[:], in0=root[:], in1=mags["b", c0][:], op=ALU.mult)
+                for a in range(PASSES):
+                    gather_words("c", a, c0, HALF, "c_words_%d" % a)
+            root = mags["a", i]
+            nc.vector.tensor_tensor(out=root[:], in0=root[:], in1=mags["b", i][:], op=ALU.mult)
             nc.scalar.activation(out=root[:], in_=root[:], func=ACT.Sqrt)
-            h_bf = work.tile([P, width * PACK], BF16, name="h_bf", tag="rounded", bufs=NB, align_bytes=64)
-            for c in range(c0, c0 + width, BLOCK):
-                o = (c - c0) * PACK
+            h_bf = work.tile([P, CHUNK * PACK], BF16, name="h_bf", tag="rounded", bufs=ROUNDED_TILES, align_bytes=64)
+            for c in range(c0, c0 + CHUNK, BLOCK):
                 nc.vector.tensor_tensor(
-                    out=h_bf[:, o : o + BLOCK * PACK].rearrange("p (j t) -> p j t", t=PACK),
-                    in0=root[:, o : o + BLOCK * PACK].rearrange("p (j t) -> p j t", t=PACK),
-                    in1=first_product("c", c), op=ALU.subtract,
+                    out=block_of(h_bf, c0, c), in0=block_of(root, c0, c), in1=first_product("c", c), op=ALU.subtract
                 )
-            h_codes = work.tile([P, width], U32, name="h_codes", align_bytes=64)
-            h_plane = work.tile([P, width], U8, name="h_plane", align_bytes=64)
+            h_codes = work.tile([P, CHUNK], U32, name="h_codes", align_bytes=64)
+            h_plane = work.tile([P, CHUNK], U8, name="h_plane", align_bytes=64)
             nc.vector.quantize_mx(out=h_codes[:].bitcast(FP8X4), scales=h_plane[:], in_=h_bf[:])
-            hq[c0] = (h_codes, h_plane)
+            h_quantised[i] = (h_codes, h_plane)
 
-        def scores(c0, width):
-            h_codes, h_plane = hq[c0]
+        def scores(i):
+            c0 = i * CHUNK
+            h_codes, h_plane = h_quantised[i]
             for g in range(GROUPS):
-                y = ypool.tile([P, PACK, width], F32, name="y%d" % g)
-                ys[g, c0] = y
-                for u in range(2):
-                    bank = psum.tile([P, 2, width], F32, name="bank_y", tag="aby", bufs=6)
-                    for e in range(2):
-                        t = 2 * u + e
-                        tcols = slice(t * P, (t + 1) * P)
+                y = work.tile([P, PACK, CHUNK], F32, name="y%d" % g)
+                scores_f32[g, i] = y
+                for t0 in range(0, PACK, 2):
+                    bank = psum.tile([P, 2, CHUNK], F32, name="bank_y", tag="shared", bufs=SHARED_BANKS)
+                    for t in (t0, t0 + 1):
+                        slice_t = slice(t * P, (t + 1) * P)
                         nc.tensor.matmul_mx(
-                            out=bank[:, e, :], lhsT=w4_codes[:, g, tcols].bitcast(FP4X4),
-                            lhsT_scale=w4_planes[:, g, tcols],
+                            out=bank[:, t - t0, :], lhsT=w4_codes[:, g, slice_t].bitcast(FP4X4),
+                            lhsT_scale=w4_planes[:, g, slice_t],
                             rhs=h_codes[:].bitcast(FP8X4), rhs_scale=h_plane[:], start=True, stop=True,
                         )
-                    for e in range(2):
-                        t = 2 * u + e
-                        if (c0, g, u) in ON_VECTOR:
-                            nc.vector.tensor_scalar(
-                                out=y[:, t, :], in0=bank[:, e, :], scalar1=bias[:, g, t : t + 1], scalar2=None, op0=ALU.add
-                            )
-                        else:
-                            nc.scalar.activation(
-                                out=y[:, t, :], in_=bank[:, e, :], func=ACT.Identity, bias=bias[:, g, t : t + 1]
-                            )
-                nc.sync.dma_start(
-                    out=out_0[g * K_PASS : (g + 1) * K_PASS, c0 : c0 + width].rearrange("(p t) j -> p t j", t=PACK),
-                    in_=y[:],
-                )
+                    for t in (t0, t0 + 1):
+                        nc.scalar.activation(
+                            out=y[:, t, :], in_=bank[:, t - t0, :], func=ACT.Identity, bias=bias[:, g, t : t + 1]
+                        )
+                rows = out_0[g * K_PASS : (g + 1) * K_PASS, c0 : c0 + CHUNK]
+                nc.sync.dma_start(out=rows.rearrange("(p t) j -> p t j", t=PACK), in_=y[:])
 
-        def planes_out(c0, width):
-            cols = slice(c0, c0 + width)
+        def score_planes(i):
+            c0 = i * CHUNK
+            cols = slice(c0, c0 + CHUNK)
             y_bf = {}
             for g in range(GROUPS):
-                y_bf[g] = work.tile([P, width * PACK], BF16, name="y_bf%d" % g, tag="rounded", bufs=NB, align_bytes=64)
-                (nc.scalar.copy if (c0, g) in ON_SCALAR else nc.vector.tensor_copy)(
-                    out=y_bf[g][:].rearrange("p (c i t) -> p c t i", i=PACK, t=PACK),
-                    in_=ys[g, c0][:].rearrange("p t (c i) -> p c t i", i=PACK),
+                y_bf[g] = work.tile(
+                    [P, CHUNK * PACK], BF16, name="y_bf%d" % g, tag="rounded", bufs=ROUNDED_TILES, align_bytes=64
+                )
+                nc.vector.tensor_copy(
+                    out=y_bf[g][:].rearrange("p (c e t) -> p c t e", e=PACK, t=PACK),
+                    in_=scores_f32[g, i][:].rearrange("p t (c e) -> p c t e", e=PACK),
                 )
             for g in range(GROUPS):
                 nc.vector.quantize_mx(
                     out=y_codes[:, g, cols].bitcast(FP8X4), scales=y_planes[:, g, cols], in_=y_bf[g][:]
                 )
-
-        def words_out(c0, width):
-            cols = slice(c0, c0 + width)
-            (nc.scalar if c0 + width == S else nc.sync).dma_start(
-                out=out_1.rearrange("g p m t -> p g (m t)")[:, :, PACK * c0 : PACK * (c0 + width)].bitcast(I32),
+            queue = nc.scalar if i == CHUNKS - 1 else nc.sync
+            queue.dma_start(
+                out=out_1.rearrange("g p m t -> p g (m t)")[:, :, PACK * c0 : PACK * (c0 + CHUNK)].bitcast(I32),
                 in_=y_codes[:, :, cols].bitcast(I32),
             )
 
-        magnitudes("a", 0, 256)
-        magnitudes("b", 0, 256)
-        magnitudes("a", 256, 256)
-        magnitudes("b", 256, 256)
-        latent(0, 256)
-        magnitudes("a", 512, 256)
-        magnitudes("b", 512, 256)
-        latent(256, 256)
-        scores(0, 256)
-        magnitudes("a", 768, 256)
-        magnitudes("b", 768, 256)
-        latent(512, 256)
-        scores(256, 256)
-        planes_out(0, 256)
-        words_out(0, 256)
-        latent(768, 256)
-        scores(512, 256)
-        planes_out(256, 256)
-        words_out(256, 256)
-        scores(768, 256)
-        planes_out(512, 256)
-        words_out(512, 256)
-        planes_out(768, 256)
-        words_out(768, 256)
-        for r in range(4):
+        stages = (magnitudes, latent, scores, score_planes)
+        for step in range(CHUNKS + len(stages) - 1):
+            for lag, stage in enumerate(stages):
+                if 0 <= step - lag < CHUNKS:
+                    stage(step - lag)
+
+        for r in range(QUAD_ROWS):
             nc.scalar.dma_start(
-                out=out_2[:, r:16:4, :].rearrange("g q c -> q g c").bitcast(I32),
-                in_=y_planes[r:P:32, :, :].bitcast(I32),
+                out=out_2[:, r:SCALE_ROWS:QUAD_ROWS, :].rearrange("g q c -> q g c").bitcast(I32),
+                in_=y_planes[r:P:QUAD, :, :].bitcast(I32),
             )

@@ -48,6 +48,10 @@ def tile_list_blend_phase_stability_kernel(
         def held(shape, dtype, name, tag=None):
             return keep.tile(shape, dtype, name=name, tag=tag or name, align_bytes=64)
 
+        warm = held([P, 1], F32, "warm")
+        nc.gpsimd.memset(warm[:], 1.0)
+        nc.scalar.activation(out=warm[:], in_=warm[:], func=ACT.Sqrt)
+
         lists = {}
         for name, source in (("b", offs2), ("a", offs), ("c", offs3)):
             lists[name] = keep.tile([P, S // ENTRIES_PER_COLUMN], U16, name="list_" + name)

from contextlib import ExitStack

import concourse.mybir as mybir

K, H, N, T, S = 1024, 512, 1024, 4096, 1024
FLOPS = 2 * (3 * K * H * S + H * N * S)

F32 = mybir.dt.float32
BF16 = mybir.dt.bfloat16
I32 = mybir.dt.int32
U32 = mybir.dt.uint32
U16 = mybir.dt.uint16
U8 = mybir.dt.uint8
FP8X4 = mybir.dt.float8_e4m3fn_x4
FP4X4 = mybir.dt.float4_e2m1fn_x4
ACT = mybir.ActivationFunctionType
ALU = mybir.AluOpType

P = 128
PACK = 4
K_PASS = P * PACK
PASSES = K // K_PASS
GROUPS = N // K_PASS
QUAD = 32
QUAD_ROWS = 4
SCALE_ROWS = 16
QUAD_ORDER = (0, 2, 1, 3)
ENTRIES_PER_COLUMN = 16
BLOCK = 128
CHUNK = 256
CHUNKS = S // CHUNK
HALF = S // 2
SHARED_BANKS = 6
C_BANKS = 2
ROUNDED_TILES = 4


def tile_list_blend_phase_stability_kernel(
    tc, tab_words, tab_scales, offs, offs2, offs3, w1, w2_words, w2_scales,
    w3_words, w3_scales, w4_words, w4_scales, b4, out_0, out_1, out_2,
):
    nc = tc.nc
    with ExitStack() as ctx:
        keep = ctx.enter_context(tc.tile_pool(name="keep", bufs=1))
        work = ctx.enter_context(tc.tile_pool(name="work", bufs=CHUNKS))
        psum = ctx.enter_context(tc.psum_pool(name="psum", bufs=1))

        def held(shape, dtype, name, tag=None):
            return keep.tile(shape, dtype, name=name, tag=tag or name, align_bytes=64)

        warm = held([P, 1], F32, "warm")
        nc.gpsimd.memset(warm[:], 1.0)
        nc.scalar.activation(out=warm[:], in_=warm[:], func=ACT.Sqrt)

        lists = {}
        for name, source in (("b", offs2), ("a", offs), ("c", offs3)):
            lists[name] = keep.tile([P, S // ENTRIES_PER_COLUMN], U16, name="list_" + name)
            nc.sync.dma_start(lists[name][:], source)

        tab_plane = held([P, T], U8, "tab_plane")
        nc.vector.memset(tab_plane[:].bitcast(I32), 0)
        w23_planes_raw = held([P, PASSES, H], U8, "w23_planes_raw", tag="c_words_0")
        nc.vector.memset(w23_planes_raw[:].rearrange("p a c -> p (a c)").bitcast(I32), 0)
        w4_planes_raw = held([P, GROUPS, K_PASS], U8, "w4_planes_raw")
        nc.vector.memset(w4_planes_raw[:].rearrange("p g c -> p (g c)").bitcast(I32), 0)
        b_plane_1 = held([P, S], U8, "b_plane_1")
        nc.vector.memset(b_plane_1[:].bitcast(I32), 0)

        tab = [held([P, T], I32, "tab%d" % a) for a in range(PASSES)]
        w1_raw = [held([P, PACK * H], F32, "w1_raw%d" % a) for a in range(PASSES)]
        w2_raw = held([P, PASSES, H // 2], I32, "w2_raw")
        w3_raw = held([P, PASSES, H], I32, "w3_raw")
        w4_raw = held([P, GROUPS, K_PASS // 2], I32, "w4_raw")
        bias = held([P, GROUPS, PACK], F32, "bias")

        def load_tab(a):
            nc.sync.dma_start(out=tab[a][:], in_=tab_words[a].rearrange("p n i -> p (n i)").bitcast(I32))

        def load_w1(a):
            rows = w1[a * K_PASS : (a + 1) * K_PASS, :]
            nc.sync.dma_start(out=w1_raw[a][:], in_=rows.rearrange("(p i) c -> p (i c)", i=PACK))

        def load_both_passes(plane, first, scales):
            for quad in QUAD_ORDER:
                start = QUAD * quad + first
                nc.sync.dma_start(
                    out=plane[start : start + PASSES * QUAD_ROWS, :].bitcast(I32),
                    in_=scales[:, QUAD_ROWS * quad : QUAD_ROWS * (quad + 1), :].bitcast(I32),
                )

        nc.sync.dma_start(out=w2_raw[:], in_=w2_words.rearrange("a p c -> p a c").bitcast(I32))
        load_both_passes(tab_plane, 0, tab_scales)
        load_tab(0)

        planes = {}
        for name in ("b", "a", "c"):
            planes[name] = held([P, S], U8, "plane_" + name)
            nc.vector.tensor_copy(planes[name][:], tab_plane[:].indirect(lists[name][:]))

        for r in range(QUAD_ROWS):
            nc.sync.dma_start(
                out=b_plane_1[r:P:QUAD, :].bitcast(I32),
                in_=planes["b"][QUAD_ROWS + r : P : QUAD, :].bitcast(I32),
            )
        load_w1(0)
        for r in range(QUAD_ROWS):
            nc.sync.dma_start(
                out=w23_planes_raw[r:P:QUAD, :, :].bitcast(I32),
                in_=w2_scales[:, r:SCALE_ROWS:QUAD_ROWS, :].rearrange("a q c -> q a c").bitcast(I32),
            )
        load_w1(1)
        load_both_passes(w23_planes_raw[:, 0, :], QUAD_ROWS, w3_scales)
        nc.sync.dma_start(out=w3_raw[:], in_=w3_words.rearrange("a p c i -> p a (c i)").bitcast(I32))
        nc.sync.dma_start(out=w4_raw[:].rearrange("p g c -> p (g c)"), in_=w4_words[0].bitcast(I32))
        load_tab(1)
        for r in range(QUAD_ROWS):
            nc.sync.dma_start(
                out=w4_planes_raw[r:P:QUAD, :, :].rearrange("p g c -> p (g c)").bitcast(I32),
                in_=w4_scales[0, r:SCALE_ROWS:QUAD_ROWS, :].bitcast(I32),
            )
        nc.sync.dma_start(out=bias[:], in_=b4.rearrange("(g p t) -> p g t", p=P, t=PACK))

        words = {}

        def gather_words(name, a, c0, width, tag):
            piece = held([P, width], U32, "words_%s%d_%d" % (name, a, c0), tag=tag)
            entries = lists[name][:, c0 // ENTRIES_PER_COLUMN : (c0 + width) // ENTRIES_PER_COLUMN]
            nc.vector.tensor_copy(piece[:], tab[a][:].bitcast(U32).indirect(entries))
            for c in range(c0, c0 + width, BLOCK):
                words[name, a, c] = piece[:, c - c0 : c - c0 + BLOCK]

        for name in ("a", "b"):
            gather_words(name, 0, 0, S, name + "_words_0")

        w1_codes = held([P, PASSES, H], U32, "w1_codes")
        w1_planes = held([P, PASSES, H], U8, "w1_planes")
        for a in range(PASSES):
            w1_bf = held([P, H * PACK], BF16, "w1_bf%d" % a)
            nc.scalar.activation(
                out=w1_bf[:].rearrange("p (t m i) -> p m i t", t=PACK, i=PACK),
                in_=w1_raw[a][:].rearrange("p (i m t) -> p m i t", i=PACK, t=PACK),
                func=ACT.Copy,
            )
            nc.vector.quantize_mx(out=w1_codes[:, a, :].bitcast(FP8X4), scales=w1_planes[:, a, :], in_=w1_bf[:])

        def deal(copy, raw, dtype, name):
            dealt = held(list(raw.shape), dtype, name)
            copy(
                out=dealt[:].rearrange("p a (t m) -> p a t m", t=PACK),
                in_=raw.rearrange("p a (m t) -> p a t m", t=PACK),
            )
            return dealt

        w2_codes = deal(nc.scalar.copy, w2_raw[:].bitcast(U16), U16, "w2_codes")
        w3_codes = deal(nc.scalar.copy, w3_raw[:].bitcast(U32), U32, "w3_codes")
        w23_planes = deal(nc.vector.tensor_copy, w23_planes_raw[:], U8, "w23_planes")
        gather_words("c", 0, 0, HALF, "c_words_0")
        w4_codes = deal(nc.scalar.copy, w4_raw[:].bitcast(U16), U16, "w4_codes")
        w4_planes = deal(nc.vector.tensor_copy, w4_planes_raw[:], U8, "w4_planes")

        def first_product(name, c):
            if name == "c":
                bank = psum.tile([P, PACK, BLOCK], F32, name="bank_c", tag="c", bufs=C_BANKS)
            else:
                bank = psum.tile([P, PACK, BLOCK], F32, name="bank_" + name, tag="shared", bufs=SHARED_BANKS)
            cols = slice(c, c + BLOCK)
            for a in range(PASSES):
                for t in range(PACK):
                    slice_t = slice(t * P, (t + 1) * P)
                    if name == "a":
                        lhs, lhs_scale = w1_codes[:, a, slice_t].bitcast(FP8X4), w1_planes[:, a, slice_t]
                        rhs_scale = planes["a"][QUAD_ROWS * a :, cols]
                    elif name == "b":
                        lhs, lhs_scale = w2_codes[:, a, slice_t].bitcast(FP4X4), w23_planes[:, a, slice_t]
                        rhs_scale = (planes["b"], b_plane_1)[a][:, cols]
                    else:
                        lhs = w3_codes[:, a, slice_t].bitcast(FP8X4)
                        lhs_scale = w23_planes[QUAD_ROWS * (a + 1) :, 0, slice_t]
                        rhs_scale = planes["c"][QUAD_ROWS * a :, cols]
                    nc.tensor.matmul_mx(
                        out=bank[:, t, :], lhsT=lhs, lhsT_scale=lhs_scale,
                        rhs=words[name, a, c].bitcast(FP8X4), rhs_scale=rhs_scale,
                        start=(a == 0 and t == 0), stop=(a == PASSES - 1 and t == PACK - 1),
                    )
            return bank[:].rearrange("p t j -> p j t")

        def block_of(tile, c0, c):
            start = (c - c0) * PACK
            return tile[:, start : start + BLOCK * PACK].rearrange("p (j t) -> p j t", t=PACK)

        mags, h_quantised, scores_f32 = {}, {}, {}
        y_codes = held([P, GROUPS, S], U32, "y_codes")
        y_planes = held([P, GROUPS, S], U8, "y_planes")

        def magnitudes(i):
            c0 = i * CHUNK
            for name in ("a", "b"):
                if c0 < HALF:
                    tag = "%s_words_1_%d" % (name, i)
                elif name == "a":
                    tag = "mag_b%d" % (i - 2)
                else:
                    tag = "b_words_1_%d" % (i - 1)
                gather_words(name, 1, c0, CHUNK, tag)
                mags[name, i] = held([P, CHUNK * PACK], F32, "mag_%s%d" % (name, i))
                for c in range(c0, c0 + CHUNK, BLOCK):
                    nc.scalar.activation(out=block_of(mags[name, i], c0, c), in_=first_product(name, c), func=ACT.Abs)

        def latent(i):
            c0 = i * CHUNK
            if c0 == 0:
                gather_words("c", 1, c0, HALF, "c_words_1")
            if c0 == HALF:
                for a in range(PASSES):
                    gather_words("c", a, c0, HALF, "c_words_%d" % a)
            root = mags["a", i]
            nc.vector.tensor_tensor(out=root[:], in0=root[:], in1=mags["b", i][:], op=ALU.mult)
            nc.scalar.activation(out=root[:], in_=root[:], func=ACT.Sqrt)
            h_bf = work.tile([P, CHUNK * PACK], BF16, name="h_bf", tag="rounded", bufs=ROUNDED_TILES, align_bytes=64)
            for c in range(c0, c0 + CHUNK, BLOCK):
                nc.vector.tensor_tensor(
                    out=block_of(h_bf, c0, c), in0=block_of(root, c0, c), in1=first_product("c", c), op=ALU.subtract
                )
            h_codes = work.tile([P, CHUNK], U32, name="h_codes", align_bytes=64)
            h_plane = work.tile([P, CHUNK], U8, name="h_plane", align_bytes=64)
            nc.vector.quantize_mx(out=h_codes[:].bitcast(FP8X4), scales=h_plane[:], in_=h_bf[:])
            h_quantised[i] = (h_codes, h_plane)

        def scores(i):
            c0 = i * CHUNK
            h_codes, h_plane = h_quantised[i]
            for g in range(GROUPS):
                y = work.tile([P, PACK, CHUNK], F32, name="y%d" % g)
                scores_f32[g, i] = y
                for t0 in range(0, PACK, 2):
                    bank = psum.tile([P, 2, CHUNK], F32, name="bank_y", tag="shared", bufs=SHARED_BANKS)
                    for t in (t0, t0 + 1):
                        slice_t = slice(t * P, (t + 1) * P)
                        nc.tensor.matmul_mx(
                            out=bank[:, t - t0, :], lhsT=w4_codes[:, g, slice_t].bitcast(FP4X4),
                            lhsT_scale=w4_planes[:, g, slice_t],
                            rhs=h_codes[:].bitcast(FP8X4), rhs_scale=h_plane[:], start=True, stop=True,
                        )
                    for t in (t0, t0 + 1):
                        nc.scalar.activation(
                            out=y[:, t, :], in_=bank[:, t - t0, :], func=ACT.Identity, bias=bias[:, g, t : t + 1]
                        )
                rows = out_0[g * K_PASS : (g + 1) * K_PASS, c0 : c0 + CHUNK]
                nc.sync.dma_start(out=rows.rearrange("(p t) j -> p t j", t=PACK), in_=y[:])

        def score_planes(i):
            c0 = i * CHUNK
            cols = slice(c0, c0 + CHUNK)
            y_bf = {}
            for g in range(GROUPS):
                y_bf[g] = work.tile(
                    [P, CHUNK * PACK], BF16, name="y_bf%d" % g, tag="rounded", bufs=ROUNDED_TILES, align_bytes=64
                )
                nc.vector.tensor_copy(
                    out=y_bf[g][:].rearrange("p (c e t) -> p c t e", e=PACK, t=PACK),
                    in_=scores_f32[g, i][:].rearrange("p t (c e) -> p c t e", e=PACK),
                )
            for g in range(GROUPS):
                nc.vector.quantize_mx(
                    out=y_codes[:, g, cols].bitcast(FP8X4), scales=y_planes[:, g, cols], in_=y_bf[g][:]
                )
            queue = nc.scalar if i == CHUNKS - 1 else nc.sync
            queue.dma_start(
                out=out_1.rearrange("g p m t -> p g (m t)")[:, :, PACK * c0 : PACK * (c0 + CHUNK)].bitcast(I32),
                in_=y_codes[:, :, cols].bitcast(I32),
            )

        stages = (magnitudes, latent, scores, score_planes)
        for step in range(CHUNKS + len(stages) - 1):
            for lag, stage in enumerate(stages):
                if 0 <= step - lag < CHUNKS:
                    stage(step - lag)

        for r in range(QUAD_ROWS):
            nc.scalar.dma_start(
                out=out_2[:, r:SCALE_ROWS:QUAD_ROWS, :].rearrange("g q c -> q g c").bitcast(I32),
                in_=y_planes[r:P:QUAD, :, :].bitcast(I32),
            )
